import numpy as np
import ml_dtypes


def mxq(x, axis, fmt="e4m3"):
    dtype, down = {"e4m3": (ml_dtypes.float8_e4m3fn, 7), "e5m2": (ml_dtypes.float8_e5m2, 14)}[fmt]
    v = np.moveaxis(np.asarray(x, np.float32).astype(ml_dtypes.bfloat16).astype(np.float64), axis, -1)
    blocks = v.reshape(v.shape[:-1] + (-1, 32))
    amax = np.abs(blocks).max(-1, keepdims=True)
    byte = np.maximum(np.where(amax > 0, np.frexp(amax)[1] - 1 + 127, 0) - down, 1)
    scale = np.exp2(byte - 127.0)
    codes = (blocks / scale).astype(np.float32).astype(dtype).astype(np.float64)
    return np.moveaxis((codes * scale).reshape(v.shape), -1, axis)


WIDE = False


def mx_kscale(k):
    if not WIDE:
        return np.ones(k)
    levels = np.array([10, -10, 5, -5, 0])
    if k % 512:
        return np.exp2(np.random.permutation(np.resize(levels, k // 32))).repeat(32)
    a = np.empty((k // 512, 16))
    for p in range(k // 512):
        a[p, :8] = np.random.permutation(np.resize(levels, 8))
        for g in range(8):
            far = levels[np.abs(levels - a[p, g]) >= 10]
            a[p, g + 8] = far[np.random.randint(len(far))]
    return np.exp2(a.ravel()).repeat(32)


def f64(x):
    return np.asarray(x).astype(np.float64)


def striped(idx):
    return np.tile(idx.reshape(-1, 16).T, (8, 1)).astype(np.uint16)


def unstriped(offs):
    return offs[:16].T.reshape(-1).astype(np.int64)


K, T, D, S, V, N = 512, 2048, 4, 512, 128, 128


def setup_inputs():
    n = np.random.standard_normal
    s = mx_kscale(K)[:, None]
    return {
        "xT": (n((K, T)) * s).astype(np.float32),
        "w": (n((K, N)) / np.sqrt(K) / s).astype(np.float32),
        "b": (0.3 * n((N, 1))).astype(np.float32),
        "offs": striped(np.random.permutation(T)[:S]),
    }


def reference(xT, w, b, offs):
    idx = unstriped(offs)
    xq = mxq(f64(xT)[:, idx], 0, "e4m3")
    y = mxq(f64(w), 0, "e4m3").T @ xq
    y = y + f64(b)
    return y.reshape(N, V, D).max(axis=2)

@@ -1,0 +1,88 @@
+from contextlib import ExitStack
+
+import concourse.mybir as mybir
+
+K, T, S, N, D = 512, 2048, 512, 128, 4
+V = S // D
+P = 128
+PACK = 4
+HALF = S // 2
+FLOPS = 2 * K * S * N
+
+F32 = mybir.dt.float32
+BF16 = mybir.dt.bfloat16
+U16 = mybir.dt.uint16
+U32 = mybir.dt.uint32
+U8 = mybir.dt.uint8
+FP8X4 = mybir.dt.float8_e4m3fn_x4
+MAX = mybir.AluOpType.max
+X = mybir.AxisListType.X
+IDENTITY = mybir.ActivationFunctionType.Identity
+
+
+def tile_picked_pool_lin_bias_sub_e_kernel(tc, xT, w, b, offs, out):
+    nc = tc.nc
+    with ExitStack() as ctx:
+        keep = ctx.enter_context(tc.tile_pool(name="keep", bufs=1))
+        psum = ctx.enter_context(tc.psum_pool(name="psum", bufs=1))
+
+        offsets = keep.tile([P, S // 16], U16, name="offsets")
+        nc.sync.dma_start(offsets[:], offs)
+
+        xT_rows = xT.rearrange("(p j) t -> p j t", j=PACK)
+        planes = []
+        for j in range(PACK):
+            plane = keep.tile([P, T], F32, name="plane%d" % j)
+            nc.sync.dma_start(plane[:], xT_rows[:, j, :])
+            planes.append(plane)
+        w_raw = keep.tile([P, PACK, N], F32, name="w_raw")
+        nc.sync.dma_start(w_raw[:], w.rearrange("(p j) n -> p j n", j=PACK))
+        bias = keep.tile([P, 1], F32, name="bias")
+        nc.scalar.dma_start(bias[:], b)
+
+        halves = []
+        for h in range(2):
+            halves.append(keep.tile([P, HALF, PACK], BF16, name="picked%d" % h, align_bytes=64))
+        for j in range(PACK):
+            for h in range(2):
+                lo = h * (HALF // 16)
+                nc.vector.tensor_copy(halves[h][:, :, j], planes[j][:].indirect(offsets[:, lo : lo + HALF // 16]))
+
+        w_grouped = keep.tile([P, N, PACK], BF16, name="w_grouped", align_bytes=64)
+        nc.scalar.copy(w_grouped[:], w_raw[:].rearrange("p j n -> p n j"))
+        w_codes = keep.tile([P, N], U32, name="w_codes", align_bytes=64)
+        w_scales = keep.tile([P, N], U8, name="w_scales", align_bytes=64)
+        nc.vector.quantize_mx(
+            out=w_codes[:].bitcast(FP8X4),
+            scales=w_scales[:],
+            in_=w_grouped[:].rearrange("p n j -> p (n j)"),
+        )
+
+        codes, scales = [], []
+        for h in range(2):
+            c = keep.tile([P, HALF], U32, name="codes%d" % h, align_bytes=64)
+            s = keep.tile([P, HALF], U8, name="scales%d" % h, align_bytes=64)
+            nc.vector.quantize_mx(
+                out=c[:].bitcast(FP8X4),
+                scales=s[:],
+                in_=halves[h][:].rearrange("p t j -> p (t j)"),
+            )
+            codes.append(c)
+            scales.append(s)
+
+        for h in range(2):
+            acc = psum.tile([P, HALF], F32, name="acc%d" % h)
+            nc.tensor.matmul_mx(
+                out=acc[:],
+                lhsT=w_codes[:].bitcast(FP8X4),
+                lhsT_scale=w_scales[:],
+                rhs=codes[h][:].bitcast(FP8X4),
+                rhs_scale=scales[h][:],
+                start=True,
+                stop=True,
+            )
+            best = keep.tile([P, HALF // D], F32, name="best%d" % h)
+            nc.vector.tensor_reduce(best[:], acc[:].rearrange("m (v d) -> m v d", d=D), axis=X, op=MAX)
+            result = keep.tile([P, HALF // D], F32, name="result%d" % h)
+            nc.scalar.activation(result[:], best[:], IDENTITY, bias=bias[:, 0:1])
+            nc.sync.dma_start(out[:, h * (HALF // D) : (h + 1) * (HALF // D)], result[:])

@@ -7,6 +7,7 @@ V = S // D
 P = 128
 PACK = 4
 HALF = S // 2
+CHUNKS = ((0, 1024), (1024, 1664), (1664, 2048))
 FLOPS = 2 * K * S * N
 
 F32 = mybir.dt.float32
@@ -18,6 +19,7 @@ FP8X4 = mybir.dt.float8_e4m3fn_x4
 MAX = mybir.AluOpType.max
 X = mybir.AxisListType.X
 IDENTITY = mybir.ActivationFunctionType.Identity
+COPY = mybir.ActivationFunctionType.Copy
 
 
 def tile_picked_pool_lin_bias_sub_e_kernel(tc, xT, w, b, offs, out):
@@ -33,23 +35,30 @@ def tile_picked_pool_lin_bias_sub_e_kernel(tc, xT, w, b, offs, out):
         planes = []
         for j in range(PACK):
             plane = keep.tile([P, T], F32, name="plane%d" % j)
-            nc.sync.dma_start(plane[:], xT_rows[:, j, :])
+            for lo, hi in ([(0, T)] if j < PACK - 1 else CHUNKS):
+                nc.sync.dma_start(plane[:, lo:hi], xT_rows[:, j, lo:hi])
             planes.append(plane)
         w_raw = keep.tile([P, PACK, N], F32, name="w_raw")
         nc.sync.dma_start(w_raw[:], w.rearrange("(p j) n -> p j n", j=PACK))
         bias = keep.tile([P, 1], F32, name="bias")
-        nc.scalar.dma_start(bias[:], b)
+        nc.gpsimd.dma_start(bias[:], b)
 
         halves = []
         for h in range(2):
             halves.append(keep.tile([P, HALF, PACK], BF16, name="picked%d" % h, align_bytes=64))
-        for j in range(PACK):
+        for j in range(PACK - 1):
             for h in range(2):
                 lo = h * (HALF // 16)
                 nc.vector.tensor_copy(halves[h][:, :, j], planes[j][:].indirect(offsets[:, lo : lo + HALF // 16]))
+        last = keep.tile([P, T], BF16, name="last")
+        nc.scalar.copy(last[:, 0:1024], planes[3][:, 0:1024])
+        nc.vector.tensor_copy(last[:, 1024:1664], planes[3][:, 1024:1664])
+        nc.vector.tensor_copy(last[:, 1664:2048], planes[3][:, 1664:2048])
+        nc.vector.tensor_copy(halves[1][:, :, 3], planes[3][:].indirect(offsets[:, HALF // 16 : S // 16]))
+        nc.scalar.activation(halves[0][:, :, 3], last[:].indirect(offsets[:, 0 : HALF // 16]), COPY)
 
         w_grouped = keep.tile([P, N, PACK], BF16, name="w_grouped", align_bytes=64)
-        nc.scalar.copy(w_grouped[:], w_raw[:].rearrange("p j n -> p n j"))
+        nc.gpsimd.tensor_scalar(w_grouped[:], w_raw[:].rearrange("p j n -> p n j"), 1.0, 0.0, mybir.AluOpType.mult, mybir.AluOpType.add)
         w_codes = keep.tile([P, N], U32, name="w_codes", align_bytes=64)
         w_scales = keep.tile([P, N], U8, name="w_scales", align_bytes=64)
         nc.vector.quantize_mx(
@@ -58,8 +67,8 @@ def tile_picked_pool_lin_bias_sub_e_kernel(tc, xT, w, b, offs, out):
             in_=w_grouped[:].rearrange("p n j -> p (n j)"),
         )
 
-        codes, scales = [], []
-        for h in range(2):
+        codes, scales = {}, {}
+        for h in (1, 0):
             c = keep.tile([P, HALF], U32, name="codes%d" % h, align_bytes=64)
             s = keep.tile([P, HALF], U8, name="scales%d" % h, align_bytes=64)
             nc.vector.quantize_mx(
@@ -67,10 +76,10 @@ def tile_picked_pool_lin_bias_sub_e_kernel(tc, xT, w, b, offs, out):
                 scales=s[:],
                 in_=halves[h][:].rearrange("p t j -> p (t j)"),
             )
-            codes.append(c)
-            scales.append(s)
+            codes[h] = c
+            scales[h] = s
 
-        for h in range(2):
+        for h in (1, 0):
             acc = psum.tile([P, HALF], F32, name="acc%d" % h)
             nc.tensor.matmul_mx(
                 out=acc[:],
@@ -81,7 +90,7 @@ def tile_picked_pool_lin_bias_sub_e_kernel(tc, xT, w, b, offs, out):
                 start=True,
                 stop=True,
             )
-            best = keep.tile([P, HALF // D], F32, name="best%d" % h)
+            best = keep.tile([P, HALF // D], F32, name="best%d" % h, tag="picked0" if h == 1 else "best", align_bytes=64)
             nc.vector.tensor_reduce(best[:], acc[:].rearrange("m (v d) -> m v d", d=D), axis=X, op=MAX)
             result = keep.tile([P, HALF // D], F32, name="result%d" % h)
             nc.scalar.activation(result[:], best[:], IDENTITY, bias=bias[:, 0:1])

@@ -41,7 +41,7 @@ def tile_picked_pool_lin_bias_sub_e_kernel(tc, xT, w, b, offs, out):
         w_raw = keep.tile([P, PACK, N], F32, name="w_raw")
         nc.sync.dma_start(w_raw[:], w.rearrange("(p j) n -> p j n", j=PACK))
         bias = keep.tile([P, 1], F32, name="bias")
-        nc.gpsimd.dma_start(bias[:], b)
+        nc.sync.dma_start(bias[:], b)
 
         halves = []
         for h in range(2):
@@ -93,5 +93,8 @@ def tile_picked_pool_lin_bias_sub_e_kernel(tc, xT, w, b, offs, out):
             best = keep.tile([P, HALF // D], F32, name="best%d" % h, tag="picked0" if h == 1 else "best", align_bytes=64)
             nc.vector.tensor_reduce(best[:], acc[:].rearrange("m (v d) -> m v d", d=D), axis=X, op=MAX)
             result = keep.tile([P, HALF // D], F32, name="result%d" % h)
-            nc.scalar.activation(result[:], best[:], IDENTITY, bias=bias[:, 0:1])
+            if h == 1:
+                nc.scalar.activation(result[:], best[:], IDENTITY, bias=bias[:, 0:1])
+            else:
+                nc.vector.tensor_scalar_add(result[:], best[:], bias[:, 0:1])
             nc.sync.dma_start(out[:, h * (HALF // D) : (h + 1) * (HALF // D)], result[:])

from contextlib import ExitStack

import concourse.mybir as mybir

K, T, S, N, D = 512, 2048, 512, 128, 4
V = S // D
P = 128
PACK = 4
HALF = S // 2
CHUNKS = ((0, 1024), (1024, 1664), (1664, 2048))
FLOPS = 2 * K * S * N

F32 = mybir.dt.float32
BF16 = mybir.dt.bfloat16
U16 = mybir.dt.uint16
U32 = mybir.dt.uint32
U8 = mybir.dt.uint8
FP8X4 = mybir.dt.float8_e4m3fn_x4
MAX = mybir.AluOpType.max
X = mybir.AxisListType.X
IDENTITY = mybir.ActivationFunctionType.Identity
COPY = mybir.ActivationFunctionType.Copy


def tile_picked_pool_lin_bias_sub_e_kernel(tc, xT, w, b, offs, out):
    nc = tc.nc
    with ExitStack() as ctx:
        keep = ctx.enter_context(tc.tile_pool(name="keep", bufs=1))
        psum = ctx.enter_context(tc.psum_pool(name="psum", bufs=1))

        offsets = keep.tile([P, S // 16], U16, name="offsets")
        nc.sync.dma_start(offsets[:], offs)

        xT_rows = xT.rearrange("(p j) t -> p j t", j=PACK)
        planes = []
        for j in range(PACK):
            plane = keep.tile([P, T], F32, name="plane%d" % j)
            for lo, hi in ([(0, T)] if j < PACK - 1 else CHUNKS):
                nc.sync.dma_start(plane[:, lo:hi], xT_rows[:, j, lo:hi])
            planes.append(plane)
        w_raw = keep.tile([P, PACK, N], F32, name="w_raw")
        nc.sync.dma_start(w_raw[:], w.rearrange("(p j) n -> p j n", j=PACK))
        bias = keep.tile([P, 1], F32, name="bias")
        nc.sync.dma_start(bias[:], b)

        halves = []
        for h in range(2):
            halves.append(keep.tile([P, HALF, PACK], BF16, name="picked%d" % h, align_bytes=64))
        for j in range(PACK - 1):
            for h in range(2):
                lo = h * (HALF // 16)
                nc.vector.tensor_copy(halves[h][:, :, j], planes[j][:].indirect(offsets[:, lo : lo + HALF // 16]))
        last = keep.tile([P, T], BF16, name="last")
        nc.scalar.copy(last[:, 0:1024], planes[3][:, 0:1024])
        nc.vector.tensor_copy(last[:, 1024:1664], planes[3][:, 1024:1664])
        nc.vector.tensor_copy(last[:, 1664:2048], planes[3][:, 1664:2048])
        nc.vector.tensor_copy(halves[1][:, :, 3], planes[3][:].indirect(offsets[:, HALF // 16 : S // 16]))
        nc.scalar.activation(halves[0][:, :, 3], last[:].indirect(offsets[:, 0 : HALF // 16]), COPY)

        w_grouped = keep.tile([P, N, PACK], BF16, name="w_grouped", align_bytes=64)
        nc.gpsimd.tensor_scalar(w_grouped[:], w_raw[:].rearrange("p j n -> p n j"), 1.0, 0.0, mybir.AluOpType.mult, mybir.AluOpType.add)
        w_codes = keep.tile([P, N], U32, name="w_codes", align_bytes=64)
        w_scales = keep.tile([P, N], U8, name="w_scales", align_bytes=64)
        nc.vector.quantize_mx(
            out=w_codes[:].bitcast(FP8X4),
            scales=w_scales[:],
            in_=w_grouped[:].rearrange("p n j -> p (n j)"),
        )

        codes, scales = {}, {}
        for h in (1, 0):
            c = keep.tile([P, HALF], U32, name="codes%d" % h, align_bytes=64)
            s = keep.tile([P, HALF], U8, name="scales%d" % h, align_bytes=64)
            nc.vector.quantize_mx(
                out=c[:].bitcast(FP8X4),
                scales=s[:],
                in_=halves[h][:].rearrange("p t j -> p (t j)"),
            )
            codes[h] = c
            scales[h] = s

        for h in (1, 0):
            acc = psum.tile([P, HALF], F32, name="acc%d" % h)
            nc.tensor.matmul_mx(
                out=acc[:],
                lhsT=w_codes[:].bitcast(FP8X4),
                lhsT_scale=w_scales[:],
                rhs=codes[h][:].bitcast(FP8X4),
                rhs_scale=scales[h][:],
                start=True,
                stop=True,
            )
            best = keep.tile([P, HALF // D], F32, name="best%d" % h, tag="picked0" if h == 1 else "best", align_bytes=64)
            nc.vector.tensor_reduce(best[:], acc[:].rearrange("m (v d) -> m v d", d=D), axis=X, op=MAX)
            result = keep.tile([P, HALF // D], F32, name="result%d" % h)
            if h == 1:
                nc.scalar.activation(result[:], best[:], IDENTITY, bias=bias[:, 0:1])
            else:
                nc.vector.tensor_scalar_add(result[:], best[:], bias[:, 0:1])
            nc.sync.dma_start(out[:, h * (HALF // D) : (h + 1) * (HALF // D)], result[:])
